import numpy as np
import ml_dtypes


def mxq(x, axis, fmt="e4m3"):
    dtype, down = {"e4m3": (ml_dtypes.float8_e4m3fn, 7), "e5m2": (ml_dtypes.float8_e5m2, 14)}[fmt]
    v = np.moveaxis(np.asarray(x, np.float32).astype(ml_dtypes.bfloat16).astype(np.float64), axis, -1)
    blocks = v.reshape(v.shape[:-1] + (-1, 32))
    amax = np.abs(blocks).max(-1, keepdims=True)
    byte = np.maximum(np.where(amax > 0, np.frexp(amax)[1] - 1 + 127, 0) - down, 1)
    scale = np.exp2(byte - 127.0)
    codes = (blocks / scale).astype(np.float32).astype(dtype).astype(np.float64)
    return np.moveaxis((codes * scale).reshape(v.shape), -1, axis)


WIDE = False


def mx_kscale(k):
    if not WIDE:
        return np.ones(k)
    levels = np.array([10, -10, 5, -5, 0])
    if k % 512:
        return np.exp2(np.random.permutation(np.resize(levels, k // 32))).repeat(32)
    a = np.empty((k // 512, 16))
    for p in range(k // 512):
        a[p, :8] = np.random.permutation(np.resize(levels, 8))
        for g in range(8):
            far = levels[np.abs(levels - a[p, g]) >= 10]
            a[p, g + 8] = far[np.random.randint(len(far))]
    return np.exp2(a.ravel()).repeat(32)


def f64(x):
    return np.asarray(x).astype(np.float64)


def striped(idx):
    return np.tile(idx.reshape(-1, 16).T, (8, 1)).astype(np.uint16)


def unstriped(offs):
    return offs[:16].T.reshape(-1).astype(np.int64)


def silu(v):
    return v / (1.0 + np.exp(-np.maximum(v, -700.0)))


K, T, E, C, N = 1536, 512, 8, 256, 256
TOP = 4


def by_expert(wq, xq):
    return np.concatenate([wq[e].T @ xq[:, e * C:(e + 1) * C] for e in range(E)], axis=1)


def setup_inputs():
    n = np.random.standard_normal
    s = mx_kscale(K)[:, None]
    deal = np.repeat(np.arange(E), C).reshape(TOP, T)[:, np.random.permutation(T)]
    deal = np.take_along_axis(deal, np.argsort(np.random.rand(TOP, T), axis=0), axis=0)
    for _ in range(8):
        s_, t_ = np.random.permutation(T).reshape(2, -1); r = np.random.randint(TOP, size=T // 2); x, y = deal[r, s_].copy(), deal[r, t_].copy()
        ok = ~((deal[:, s_] == y).any(0) | (deal[:, t_] == x).any(0)); deal[r[ok], s_[ok]] = y[ok]; deal[r[ok], t_[ok]] = x[ok]
    order = np.lexsort((np.random.rand(TOP * T), deal.reshape(-1)))
    slot_token = order % T; pos = np.empty(TOP * T, np.int64); pos[order] = np.arange(TOP * T); pos = pos.reshape(TOP, T)
    g = np.random.uniform(0.5, 1.5, (TOP, T)); g = g / g.sum(0)
    return {
        "xT": (n((K, T)) * s).astype(np.float32),
        "w": (n((E + 1, K, N)) / np.sqrt(K) / s[None]).astype(np.float32),
        "b": (0.3 * n((N, E + 1))).astype(np.float32),
        "gate": np.stack([np.tile(r, (N, 1)) for r in g]).astype(np.float32),
        "offs": striped(slot_token),
        "pos1": striped(pos[0]),
        "pos2": striped(pos[1]),
        "pos3": striped(pos[2]),
        "pos4": striped(pos[3]),
    }


def reference(xT, w, b, gate, offs, pos1, pos2, pos3, pos4):
    idx = unstriped(offs)
    wq = mxq(f64(w), 1, "e4m3")
    xs = mxq(f64(xT), 0, "e4m3")
    ys = silu((wq[E].T @ xs) + f64(b)[:, E:])
    xq = mxq(f64(xT)[:, idx], 0, "e4m3")
    y = by_expert(wq, xq)
    y = silu(y + np.repeat(f64(b)[:, :E], C, axis=1))
    return ys + sum(f64(gate[r]) * y[:, unstriped(p)] for r, p in enumerate((pos1, pos2, pos3, pos4)))

@@ -1,0 +1,273 @@
+from contextlib import ExitStack
+
+import concourse.mybir as mybir
+from concourse.masks import make_identity
+
+K, T, E, C, N, TOP = 1536, 512, 8, 256, 256, 4
+FLOPS = 2 * K * N * (E * C + T)
+
+F32 = mybir.dt.float32
+BF16 = mybir.dt.bfloat16
+U32 = mybir.dt.uint32
+U16 = mybir.dt.uint16
+U8 = mybir.dt.uint8
+FP8X4 = mybir.dt.float8_e4m3fn_x4
+SILU = mybir.ActivationFunctionType.Silu
+MULT = mybir.AluOpType.mult
+ADD = mybir.AluOpType.add
+
+P = 128
+PACK = 4
+K_PASS = P * PACK
+PASSES = K // K_PASS
+PLANES = 2 * PASSES
+SLOTS = E * C
+GROUP = 2 * C
+HALVES = N // P
+SHARED = E
+W_BUFS = 4
+G_RING = 3
+S_RING = 2
+FIRST_SPLIT = 6
+TOK_AT = [2,3,11]
+PER_STEP = [0,0,4,0,0,2,3,2,3,2,2,1,2,2,2,6,1,1]
+ON_GPSIMD = [0,5,7,13,15,20,21,22,23,27]
+ON_VECTOR = [16,21,27,30]
+LAG = [3,3,2,2,2,2,3,3,3]
+WIDEST = 1024
+PICKED = 6
+
+
+def tile_moe_shr_lin_silu_kernel(tc, xT, w, b, gate, offs, pos1, pos2, pos3, pos4, out):
+    nc = tc.nc
+    units = [(s, g) for g in range(PASSES) for s in (0, 1)] + [(s, g) for s in (2, 3) for g in range(PASSES)]
+    steps = units + [None] * 3
+    for g in range(PASSES):
+        steps.insert(TOK_AT[g], (SHARED, g))
+    w_tasks = [(e, g, 0, N if e < FIRST_SPLIT else P) for e in range(E) for g in range(PASSES)]
+    w_tasks += [(e, g, P, N) for e in range(FIRST_SPLIT, E) for g in range(PASSES)]
+    w_tasks += [(SHARED, g, 0, N) for g in range(PASSES)]
+    assert sum(PER_STEP) == len(w_tasks)
+    tasks_of = [w_tasks[sum(PER_STEP[:i]) : sum(PER_STEP[: i + 1])] for i in range(len(steps))]
+    task_at, widths = {}, []
+    for i, step in enumerate(steps):
+        widths.append(GROUP if step else 0)
+        for task in tasks_of[i]:
+            task_at[task] = (i, widths[i])
+            widths[i] += task[3] - task[2]
+    code_at = [sum(widths[:i]) for i in range(len(steps))]
+
+    with ExitStack() as ctx:
+        keep = ctx.enter_context(tc.tile_pool(name="keep", bufs=1))
+        stage = ctx.enter_context(tc.tile_pool(name="stage", bufs=PLANES))
+        wraw_pool = ctx.enter_context(tc.tile_pool(name="wraw", bufs=W_BUFS))
+        ring = ctx.enter_context(tc.tile_pool(name="ring", bufs=3))
+        psum = ctx.enter_context(tc.psum_pool(name="psum", bufs=5))
+        turn = ctx.enter_context(tc.psum_pool(name="turn", bufs=1))
+
+        offs_sb = keep.tile([P, SLOTS // 16], U16, name="offs_sb")
+        pos_sb = [keep.tile([P, T // 16], U16, name="pos_sb%d" % r) for r in range(TOP)]
+        bias = keep.tile([P, HALVES, E + 1], F32, name="bias")
+        pairs = keep.tile([P, PLANES * T * 2], BF16, name="pairs", align_bytes=64)
+        gathered = keep.tile([P, G_RING, 2, GROUP], U32, name="gathered")
+        laid = keep.tile([P, S_RING, max(widths) * PACK], BF16, name="laid", align_bytes=64)
+        codes = keep.tile([P, sum(widths)], U32, name="codes", align_bytes=64)
+        scales = keep.tile([P, sum(widths)], U8, name="scales", align_bytes=64)
+        y = [keep.tile([P, SLOTS], F32, name="y%d" % h) for h in range(HALVES)]
+        ys = keep.tile([P, HALVES, T], F32, name="ys")
+        ident = keep.tile([P, P], F32, name="ident")
+        warm = keep.tile([P, 2], F32, name="warm")
+
+        x_raw, w_raw, gates = {}, {}, {}
+
+        def plane_start(q):
+            return (PLANES - 1 - q) * T
+
+        def load_x(q):
+            g, u = divmod(q, 2)
+            x_raw[q] = stage.tile([P, 2, T], F32, name="stage")
+            rows = xT[g * K_PASS : (g + 1) * K_PASS, :].rearrange("(p j) t -> p j t", j=PACK)
+            nc.sync.dma_start(out=x_raw[q][:], in_=rows[:, 2 * u : 2 * u + 2, :])
+
+        def load_w(e):
+            w_raw[e] = wraw_pool.tile([P, PASSES, PACK, N], F32, name="w_raw")
+            nc.sync.dma_start(out=w_raw[e][:], in_=w[e].rearrange("(g p j) n -> p g j n", p=P, j=PACK))
+
+        def load_gate(h):
+            for a in range(TOP // 2):
+                gates[h, a] = stage.tile([P, 2, T], F32, name="stage")
+                nc.sync.dma_start(
+                    out=gates[h, a][:], in_=gate[2 * a : 2 * a + 2, h * P : (h + 1) * P, :].rearrange("r p t -> p r t")
+                )
+
+        def round_plane(q, copy):
+            dst = pairs[:, 2 * plane_start(q) : 2 * (plane_start(q) + T)].rearrange("p (t e) -> p t e", e=2)
+            copy(out=dst, in_=x_raw[q][:].rearrange("p e t -> p t e"))
+
+        def gather(i, u):
+            s, g = steps[i]
+            q = 2 * g + u
+            width, count = (T, C) if q == 0 else (2 * T, GROUP)
+            window = pairs[:, 2 * plane_start(q) : 2 * (plane_start(q) + width)].bitcast(U32)
+            for m in range(0, GROUP, count):
+                cols = slice((s * GROUP + m) // 16, (s * GROUP + m + count) // 16)
+                nc.vector.tensor_copy(out=gathered[:, units.index(steps[i]) % G_RING, u, m : m + count], in_=window.indirect(offs_sb[:, cols]))
+
+        def lay_columns(i):
+            s, g = steps[i]
+            if s == SHARED:
+                both = pairs[:, 2 * plane_start(2 * g + 1) : 2 * (plane_start(2 * g) + T)].bitcast(F32)
+                src = both.rearrange("p (u t) -> p t u", u=2)[:, :, ::-1]
+            else:
+                src = gathered[:, units.index(steps[i]) % G_RING].bitcast(F32).rearrange("p u m -> p m u")
+            dst = laid[:, i % S_RING, : GROUP * PACK].bitcast(F32).rearrange("p (m u) -> p m u", u=2)
+            nc.scalar.copy(out=dst, in_=src)
+
+        def round_w(i, task):
+            e, g, n0, n1 = task
+            at = task_at[task][1] * PACK
+            dst, src = laid[:, i % S_RING, at : at + (n1 - n0) * PACK], w_raw[e][:, g, :, n0:n1]
+            if w_tasks.index(task) in ON_GPSIMD:
+                nc.gpsimd.tensor_scalar(
+                    out=dst.rearrange("p (n j) -> p n j", j=PACK),
+                    in0=src.rearrange("p j n -> p n j"),
+                    scalar1=1.0,
+                    scalar2=0.0,
+                    op0=MULT,
+                    op1=ADD,
+                )
+            else:
+                copy = nc.vector.tensor_copy if w_tasks.index(task) in ON_VECTOR else nc.scalar.copy
+                copy(
+                    out=dst.rearrange("p (c i j) -> p c j i", i=4, j=PACK),
+                    in_=src.rearrange("p j (c i) -> p c j i", i=4),
+                )
+
+        def quantize(i):
+            done = 0
+            while done < widths[i]:
+                piece = max(n for n in (P, N, 2 * N, WIDEST) if n <= widths[i] - done)
+                cols = slice(code_at[i] + done, code_at[i] + done + piece)
+                nc.vector.quantize_mx(
+                    out=codes[:, cols].bitcast(FP8X4),
+                    scales=scales[:, cols],
+                    in_=laid[:, i % S_RING, done * PACK : (done + piece) * PACK],
+                )
+                done += piece
+
+        def w_task(e, g, h):
+            return [t for t in w_tasks if t[:2] == (e, g) and t[2] <= h * P < t[3]][0]
+
+        def multiply(e, h):
+            width = T if e == SHARED else C
+            acc = psum.tile([P, width], F32, name="acc")
+            for g in range(PASSES):
+                task = w_task(e, g, h)
+                at = code_at[task_at[task][0]] + task_at[task][1] + h * P - task[2]
+                rows = slice(at, at + P)
+                at = code_at[steps.index((SHARED, g))] if e == SHARED else code_at[steps.index((e // 2, g))] + e % 2 * C
+                cols = slice(at, at + width)
+                nc.tensor.matmul_mx(
+                    out=acc[:],
+                    lhsT=codes[:, rows].bitcast(FP8X4),
+                    lhsT_scale=scales[:, rows],
+                    rhs=codes[:, cols].bitcast(FP8X4),
+                    rhs_scale=scales[:, cols],
+                    start=(g == 0),
+                    stop=(g == PASSES - 1),
+                )
+            dst = ys[:, h, :] if e == SHARED else y[h][:, e * C : (e + 1) * C]
+            nc.scalar.activation(out=dst, in_=acc[:], func=SILU, bias=bias[:, h, e : e + 1])
+
+        def fetch(h, r):
+            picked = ring.tile([P, T], F32, name="picked", bufs=PICKED)
+            nc.vector.tensor_tensor(picked[:], y[h][:].indirect(pos_sb[r][:]), gates[h, r // 2][:, r % 2, :], MULT)
+            return picked
+
+        def add(first, second, name="total"):
+            total = ring.tile([P, T], F32, name=name, bufs=1)
+            nc.vector.tensor_tensor(total[:], first, second, ADD)
+            return total
+
+        def sum_on_tensor(terms, h):
+            turned = turn.tile([P, T], F32, name="turned")
+            for m in range(0, T, P):
+                for k, term in enumerate(terms):
+                    nc.tensor.matmul(
+                        turned[:, m : m + P],
+                        lhsT=term[:, m : m + P],
+                        rhs=ident[:],
+                        start=(k == 0),
+                        stop=(k == len(terms) - 1),
+                        is_transpose=True,
+                    )
+            turned_sb = ring.tile([P, T], F32, name="turned_sb", bufs=1)
+            nc.scalar.copy(out=turned_sb[:], in_=turned[:])
+            back = turn.tile([P, T], F32, name="back%d" % h)
+            for m in range(0, T, P):
+                nc.tensor.transpose(back[:, m : m + P], turned_sb[:, m : m + P], ident[:])
+            return back
+
+        make_identity(nc, ident[:])
+        nc.gpsimd.memset(warm[:, 0:1], 0.0)
+        nc.scalar.activation(out=warm[:, 1:2], in_=warm[:, 0:1], func=SILU)
+        load_x(0)
+        nc.sync.dma_start(offs_sb[:], offs)
+        for q in range(1, PLANES):
+            load_x(q)
+        load_w(0)
+        nc.sync.dma_start(out=bias[:], in_=b.rearrange("(h p) e -> p h e", p=P))
+        load_w(1)
+        for r, pos in enumerate((pos1, pos2, pos3, pos4)):
+            nc.sync.dma_start(pos_sb[r][:], pos)
+        for e in range(2, W_BUFS):
+            load_w(e)
+
+        round_plane(0, nc.vector.tensor_copy)
+        for q in (1, 2, 3):
+            round_plane(q, nc.scalar.copy)
+        last = len(steps) - 1
+        due = {}
+        for e in range(E + 1):
+            for h in range(HALVES):
+                ready = max(
+                    max(task_at[w_task(e, g, h)][0], steps.index((e if e == SHARED else e // 2, g))) for g in range(PASSES)
+                )
+                due[e, h] = min(ready + LAG[e], last)
+        partial = {}
+        for i, step in enumerate(steps):
+            for task in tasks_of[i]:
+                round_w(i, task)
+                e = task[0]
+                if task[1] == PASSES - 1 and task[3] == N and e + W_BUFS <= SHARED:
+                    if e + W_BUFS == SHARED:
+                        load_gate(0)
+                    load_w(e + W_BUFS)
+                    if e + W_BUFS == SHARED:
+                        load_gate(1)
+            if step in units:
+                gather(i, 0)
+                gather(i, 1)
+            if step:
+                lay_columns(i)
+            quantize(i)
+            if i < 2:
+                round_plane(4 + i, nc.scalar.copy)
+            for h in range(HALVES):
+                for e in range(E + 1):
+                    if due[e, h] == i:
+                        multiply(e, h)
+            if i == max(due[e, 0] for e in range(E)):
+                first = [fetch(0, r) for r in range(TOP)]
+
+        back = sum_on_tensor(first + [ys[:, 0, :]], 0)
+        result = ring.tile([P, T], F32, name="result", bufs=2)
+        nc.scalar.copy(out=result[:], in_=back[:])
+        nc.sync.dma_start(out=out[0:P, :], in_=result[:])
+        back = sum_on_tensor([fetch(1, 0), fetch(1, 1), ys[:, 1, :]], 1)
+        total = add(fetch(1, 2)[:], fetch(1, 3)[:])
+        result = ring.tile([P, T], F32, name="result", bufs=2)
+        for m in range(0, T, T // 2):
+            cols = slice(m, m + T // 2)
+            nc.vector.tensor_tensor(result[:, cols], back[:, cols], total[:, cols], ADD)
+            nc.sync.dma_start(out=out[P : 2 * P, cols], in_=result[:, cols])

@@ -21,81 +21,77 @@ PACK = 4
 K_PASS = P * PACK
 PASSES = K // K_PASS
 PLANES = 2 * PASSES
-SLOTS = E * C
 GROUP = 2 * C
 HALVES = N // P
 SHARED = E
-W_BUFS = 4
-G_RING = 3
-S_RING = 2
-FIRST_SPLIT = 6
-TOK_AT = [2,3,11]
-PER_STEP = [0,0,4,0,0,2,3,2,3,2,2,1,2,2,2,6,1,1]
-ON_GPSIMD = [0,5,7,13,15,20,21,22,23,27]
-ON_VECTOR = [16,21,27,30]
-LAG = [3,3,2,2,2,2,3,3,3]
-WIDEST = 1024
-PICKED = 6
+RAW_BUFS = 14
+L_RING = 5
+W_RING = 3
+VECTOR_BUFS = 26
+FIRST_SPLIT = 8
+UNITS = [[0,0],[1,0],[0,1],[0,2],[1,1],[2,0],[1,2],[3,0],[2,1],[2,2],[3,2],[3,1]]
+W_SIZE = [512,512,512,512,512,512,512,512,512,512,512,512,512,256]
+ON_GPSIMD = [0,1,3,4,5,7,8,10,11,12]
+V_ORDER = "G0 G1 G2 L0 G3 G4 L1 W0 W1 G5 W2 L2 G6 W3 W4 L3 G7 L4 L5 W5 L6 G8 W6 W7 W8 G9 G10 L7 W9 W10 G11 L8 W11 L9 L10 L11 L12 L13 W12 F0 F1 L14 W13 F2 F3"
+LAG = 3
+GATE_AT = [21,27]
 
 
 def tile_moe_shr_lin_silu_kernel(tc, xT, w, b, gate, offs, pos1, pos2, pos3, pos4, out):
     nc = tc.nc
-    units = [(s, g) for g in range(PASSES) for s in (0, 1)] + [(s, g) for s in (2, 3) for g in range(PASSES)]
-    steps = units + [None] * 3
-    for g in range(PASSES):
-        steps.insert(TOK_AT[g], (SHARED, g))
-    w_tasks = [(e, g, 0, N if e < FIRST_SPLIT else P) for e in range(E) for g in range(PASSES)]
-    w_tasks += [(e, g, P, N) for e in range(FIRST_SPLIT, E) for g in range(PASSES)]
-    w_tasks += [(SHARED, g, 0, N) for g in range(PASSES)]
-    assert sum(PER_STEP) == len(w_tasks)
-    tasks_of = [w_tasks[sum(PER_STEP[:i]) : sum(PER_STEP[: i + 1])] for i in range(len(steps))]
-    task_at, widths = {}, []
-    for i, step in enumerate(steps):
-        widths.append(GROUP if step else 0)
-        for task in tasks_of[i]:
-            task_at[task] = (i, widths[i])
-            widths[i] += task[3] - task[2]
-    code_at = [sum(widths[:i]) for i in range(len(steps))]
+    routed = [tuple(u) for u in UNITS]
+    steps = routed + [(SHARED, g) for g in range(PASSES)]
+    pieces = [(e, g, 0, N if e < FIRST_SPLIT else P) for e in range(E) for g in range(PASSES)]
+    pieces += [(e, g, P, N) for e in range(FIRST_SPLIT, E) for g in range(PASSES)]
+    pieces += [(SHARED, g, 0, N) for g in range(PASSES)]
+    place, width = {}, [0] * len(W_SIZE)
+    j = 0
+    for piece in pieces:
+        while width[j] + piece[3] - piece[2] > W_SIZE[j]:
+            j += 1
+        place[piece] = (j, width[j])
+        width[j] += piece[3] - piece[2]
 
     with ExitStack() as ctx:
         keep = ctx.enter_context(tc.tile_pool(name="keep", bufs=1))
-        stage = ctx.enter_context(tc.tile_pool(name="stage", bufs=PLANES))
-        wraw_pool = ctx.enter_context(tc.tile_pool(name="wraw", bufs=W_BUFS))
-        ring = ctx.enter_context(tc.tile_pool(name="ring", bufs=3))
-        psum = ctx.enter_context(tc.psum_pool(name="psum", bufs=5))
-        turn = ctx.enter_context(tc.psum_pool(name="turn", bufs=1))
+        raw_pool = ctx.enter_context(tc.tile_pool(name="raw", bufs=RAW_BUFS))
+        sum_pool = ctx.enter_context(tc.tile_pool(name="sums", bufs=2))
+        vector_pool = ctx.enter_context(tc.tile_pool(name="vector", bufs=VECTOR_BUFS))
+        psum = ctx.enter_context(tc.psum_pool(name="psum", bufs=8))
 
-        offs_sb = keep.tile([P, SLOTS // 16], U16, name="offs_sb")
+        offs_sb = keep.tile([P, E * C // 16], U16, name="offs_sb")
         pos_sb = [keep.tile([P, T // 16], U16, name="pos_sb%d" % r) for r in range(TOP)]
         bias = keep.tile([P, HALVES, E + 1], F32, name="bias")
         pairs = keep.tile([P, PLANES * T * 2], BF16, name="pairs", align_bytes=64)
-        gathered = keep.tile([P, G_RING, 2, GROUP], U32, name="gathered")
-        laid = keep.tile([P, S_RING, max(widths) * PACK], BF16, name="laid", align_bytes=64)
-        codes = keep.tile([P, sum(widths)], U32, name="codes", align_bytes=64)
-        scales = keep.tile([P, sum(widths)], U8, name="scales", align_bytes=64)
-        y = [keep.tile([P, SLOTS], F32, name="y%d" % h) for h in range(HALVES)]
+        y = [keep.tile([P, E * C], F32, name="y%d" % h) for h in range(HALVES)]
         ys = keep.tile([P, HALVES, T], F32, name="ys")
+        l_ring = keep.tile([P, L_RING, GROUP * PACK], BF16, name="l_ring", align_bytes=64)
+        w_ring = keep.tile([P, W_RING, GROUP * PACK], BF16, name="w_ring", align_bytes=64)
         ident = keep.tile([P, P], F32, name="ident")
         warm = keep.tile([P, 2], F32, name="warm")
 
-        x_raw, w_raw, gates = {}, {}, {}
+        x_raw, w_raw, gates, gathered, staged, coded = {}, {}, {}, {}, {}, {}
+
+        def vector_tile(shape, dtype):
+            return vector_pool.tile(shape, dtype, name="vector_out", align_bytes=64)
 
         def plane_start(q):
             return (PLANES - 1 - q) * T
 
         def load_x(q):
             g, u = divmod(q, 2)
-            x_raw[q] = stage.tile([P, 2, T], F32, name="stage")
+            x_raw[q] = raw_pool.tile([P, 2, T], F32, name="raw")
             rows = xT[g * K_PASS : (g + 1) * K_PASS, :].rearrange("(p j) t -> p j t", j=PACK)
             nc.sync.dma_start(out=x_raw[q][:], in_=rows[:, 2 * u : 2 * u + 2, :])
 
-        def load_w(e):
-            w_raw[e] = wraw_pool.tile([P, PASSES, PACK, N], F32, name="w_raw")
-            nc.sync.dma_start(out=w_raw[e][:], in_=w[e].rearrange("(g p j) n -> p g j n", p=P, j=PACK))
+        def load_w(e, g):
+            w_raw[e, g] = raw_pool.tile([P, PACK, N], F32, name="raw")
+            rows = w[e, g * K_PASS : (g + 1) * K_PASS, :]
+            nc.sync.dma_start(out=w_raw[e, g][:], in_=rows.rearrange("(p j) n -> p j n", j=PACK))
 
         def load_gate(h):
             for a in range(TOP // 2):
-                gates[h, a] = stage.tile([P, 2, T], F32, name="stage")
+                gates[h, a] = raw_pool.tile([P, 2, T], F32, name="raw")
                 nc.sync.dma_start(
                     out=gates[h, a][:], in_=gate[2 * a : 2 * a + 2, h * P : (h + 1) * P, :].rearrange("r p t -> p r t")
                 )
@@ -106,73 +102,80 @@ def tile_moe_shr_lin_silu_kernel(tc, xT, w, b, gate, offs, pos1, pos2, pos3, pos
 
         def gather(i, u):
             s, g = steps[i]
+            if u == 0:
+                gathered[i] = vector_tile([P, 2, GROUP], U32)
             q = 2 * g + u
-            width, count = (T, C) if q == 0 else (2 * T, GROUP)
-            window = pairs[:, 2 * plane_start(q) : 2 * (plane_start(q) + width)].bitcast(U32)
+            columns, count = (T, C) if q == 0 else (2 * T, GROUP)
+            window = pairs[:, 2 * plane_start(q) : 2 * (plane_start(q) + columns)].bitcast(U32)
             for m in range(0, GROUP, count):
                 cols = slice((s * GROUP + m) // 16, (s * GROUP + m + count) // 16)
-                nc.vector.tensor_copy(out=gathered[:, units.index(steps[i]) % G_RING, u, m : m + count], in_=window.indirect(offs_sb[:, cols]))
+                nc.vector.tensor_copy(out=gathered[i][:, u, m : m + count], in_=window.indirect(offs_sb[:, cols]))
 
-        def lay_columns(i):
+        def stage_w(j):
+            staged["W", j] = w_ring[:, j % W_RING, : width[j] * PACK]
+            for piece in [piece for piece in pieces if place[piece][0] == j]:
+                e, g, n0, n1 = piece
+                at = place[piece][1] * PACK
+                dst, src = staged["W", j][:, at : at + (n1 - n0) * PACK], w_raw[e, g][:, :, n0:n1]
+                if j in ON_GPSIMD and place[piece][1] >= N:
+                    nc.gpsimd.tensor_scalar(
+                        out=dst.rearrange("p (n j) -> p n j", j=PACK),
+                        in0=src.rearrange("p j n -> p n j"),
+                        scalar1=1.0,
+                        scalar2=0.0,
+                        op0=MULT,
+                        op1=ADD,
+                    )
+                else:
+                    nc.scalar.copy(
+                        out=dst.rearrange("p (c i j) -> p c j i", i=4, j=PACK),
+                        in_=src.rearrange("p j (c i) -> p c j i", i=4),
+                    )
+
+        def stage_columns(i):
             s, g = steps[i]
+            staged["L", i] = l_ring[:, i % L_RING, :]
             if s == SHARED:
                 both = pairs[:, 2 * plane_start(2 * g + 1) : 2 * (plane_start(2 * g) + T)].bitcast(F32)
                 src = both.rearrange("p (u t) -> p t u", u=2)[:, :, ::-1]
             else:
-                src = gathered[:, units.index(steps[i]) % G_RING].bitcast(F32).rearrange("p u m -> p m u")
-            dst = laid[:, i % S_RING, : GROUP * PACK].bitcast(F32).rearrange("p (m u) -> p m u", u=2)
-            nc.scalar.copy(out=dst, in_=src)
+                src = gathered[i][:].bitcast(F32).rearrange("p u m -> p m u")
+            nc.scalar.copy(out=staged["L", i].bitcast(F32).rearrange("p (m u) -> p m u", u=2), in_=src)
 
-        def round_w(i, task):
-            e, g, n0, n1 = task
-            at = task_at[task][1] * PACK
-            dst, src = laid[:, i % S_RING, at : at + (n1 - n0) * PACK], w_raw[e][:, g, :, n0:n1]
-            if w_tasks.index(task) in ON_GPSIMD:
-                nc.gpsimd.tensor_scalar(
-                    out=dst.rearrange("p (n j) -> p n j", j=PACK),
-                    in0=src.rearrange("p j n -> p n j"),
-                    scalar1=1.0,
-                    scalar2=0.0,
-                    op0=MULT,
-                    op1=ADD,
-                )
-            else:
-                copy = nc.vector.tensor_copy if w_tasks.index(task) in ON_VECTOR else nc.scalar.copy
-                copy(
-                    out=dst.rearrange("p (c i j) -> p c j i", i=4, j=PACK),
-                    in_=src.rearrange("p j (c i) -> p c j i", i=4),
-                )
+        def operand(key, at, columns):
+            total = staged[key].shape[1] // PACK
+            codes = coded[key][:, 4 * at : 4 * (at + columns)].bitcast(FP8X4)
+            return codes, coded[key][:, 4 * total + at : 4 * total + at + columns]
 
-        def quantize(i):
+        def quantize(key):
+            total = staged[key].shape[1] // PACK
+            coded[key] = vector_tile([P, 5 * total], U8)
             done = 0
-            while done < widths[i]:
-                piece = max(n for n in (P, N, 2 * N, WIDEST) if n <= widths[i] - done)
-                cols = slice(code_at[i] + done, code_at[i] + done + piece)
-                nc.vector.quantize_mx(
-                    out=codes[:, cols].bitcast(FP8X4),
-                    scales=scales[:, cols],
-                    in_=laid[:, i % S_RING, done * PACK : (done + piece) * PACK],
-                )
-                done += piece
+            while done < total:
+                columns = max(n for n in (P, N, GROUP) if n <= total - done)
+                codes, scales = operand(key, done, columns)
+                nc.vector.quantize_mx(out=codes, scales=scales, in_=staged[key][:, done * PACK : (done + columns) * PACK])
+                done += columns
 
-        def w_task(e, g, h):
-            return [t for t in w_tasks if t[:2] == (e, g) and t[2] <= h * P < t[3]][0]
+        def piece_of(e, g, h):
+            return [piece for piece in pieces if piece[:2] == (e, g) and piece[2] <= h * P < piece[3]][0]
 
         def multiply(e, h):
-            width = T if e == SHARED else C
-            acc = psum.tile([P, width], F32, name="acc")
+            columns = T if e == SHARED else C
+            acc = psum.tile([P, columns], F32, name="bank")
             for g in range(PASSES):
-                task = w_task(e, g, h)
-                at = code_at[task_at[task][0]] + task_at[task][1] + h * P - task[2]
-                rows = slice(at, at + P)
-                at = code_at[steps.index((SHARED, g))] if e == SHARED else code_at[steps.index((e // 2, g))] + e % 2 * C
-                cols = slice(at, at + width)
+                piece = piece_of(e, g, h)
+                w_codes, w_scales = operand(("W", place[piece][0]), place[piece][1] + h * P - piece[2], P)
+                if e == SHARED:
+                    x_codes, x_scales = operand(("L", steps.index((SHARED, g))), 0, T)
+                else:
+                    x_codes, x_scales = operand(("L", steps.index((e // 2, g))), e % 2 * C, C)
                 nc.tensor.matmul_mx(
                     out=acc[:],
-                    lhsT=codes[:, rows].bitcast(FP8X4),
-                    lhsT_scale=scales[:, rows],
-                    rhs=codes[:, cols].bitcast(FP8X4),
-                    rhs_scale=scales[:, cols],
+                    lhsT=w_codes,
+                    lhsT_scale=w_scales,
+                    rhs=x_codes,
+                    rhs_scale=x_scales,
                     start=(g == 0),
                     stop=(g == PASSES - 1),
                 )
@@ -180,17 +183,12 @@ def tile_moe_shr_lin_silu_kernel(tc, xT, w, b, gate, offs, pos1, pos2, pos3, pos
             nc.scalar.activation(out=dst, in_=acc[:], func=SILU, bias=bias[:, h, e : e + 1])
 
         def fetch(h, r):
-            picked = ring.tile([P, T], F32, name="picked", bufs=PICKED)
+            picked = vector_tile([P, T], F32)
             nc.vector.tensor_tensor(picked[:], y[h][:].indirect(pos_sb[r][:]), gates[h, r // 2][:, r % 2, :], MULT)
             return picked
 
-        def add(first, second, name="total"):
-            total = ring.tile([P, T], F32, name=name, bufs=1)
-            nc.vector.tensor_tensor(total[:], first, second, ADD)
-            return total
-
-        def sum_on_tensor(terms, h):
-            turned = turn.tile([P, T], F32, name="turned")
+        def sum_on_tensor(terms):
+            turned = psum.tile([P, T], F32, name="bank")
             for m in range(0, T, P):
                 for k, term in enumerate(terms):
                     nc.tensor.matmul(
@@ -201,9 +199,9 @@ def tile_moe_shr_lin_silu_kernel(tc, xT, w, b, gate, offs, pos1, pos2, pos3, pos
                         stop=(k == len(terms) - 1),
                         is_transpose=True,
                     )
-            turned_sb = ring.tile([P, T], F32, name="turned_sb", bufs=1)
+            turned_sb = sum_pool.tile([P, T], F32, name="sum_sb")
             nc.scalar.copy(out=turned_sb[:], in_=turned[:])
-            back = turn.tile([P, T], F32, name="back%d" % h)
+            back = psum.tile([P, T], F32, name="bank")
             for m in range(0, T, P):
                 nc.tensor.transpose(back[:, m : m + P], turned_sb[:, m : m + P], ident[:])
             return back
@@ -215,58 +213,59 @@ def tile_moe_shr_lin_silu_kernel(tc, xT, w, b, gate, offs, pos1, pos2, pos3, pos
         nc.sync.dma_start(offs_sb[:], offs)
         for q in range(1, PLANES):
             load_x(q)
-        load_w(0)
-        nc.sync.dma_start(out=bias[:], in_=b.rearrange("(h p) e -> p h e", p=P))
-        load_w(1)
-        for r, pos in enumerate((pos1, pos2, pos3, pos4)):
-            nc.sync.dma_start(pos_sb[r][:], pos)
-        for e in range(2, W_BUFS):
-            load_w(e)
+        for m in range((E + 1) * PASSES):
+            load_w(*divmod(m, PASSES))
+            if m == PASSES - 1:
+                nc.sync.dma_start(out=bias[:], in_=b.rearrange("(h p) e -> p h e", p=P))
+                for r, pos in enumerate((pos1, pos2, pos3, pos4)):
+                    nc.sync.dma_start(pos_sb[r][:], pos)
+            for h in range(HALVES):
+                if m + 1 == GATE_AT[h]:
+                    load_gate(h)
 
-        round_plane(0, nc.vector.tensor_copy)
-        for q in (1, 2, 3):
-            round_plane(q, nc.scalar.copy)
-        last = len(steps) - 1
+        v_order = [(word[0], int(word[1:])) for word in V_ORDER.split()]
+        quantized = [key for key in v_order if key[0] in "WL"]
         due = {}
         for e in range(E + 1):
             for h in range(HALVES):
-                ready = max(
-                    max(task_at[w_task(e, g, h)][0], steps.index((e if e == SHARED else e // 2, g))) for g in range(PASSES)
-                )
-                due[e, h] = min(ready + LAG[e], last)
-        partial = {}
-        for i, step in enumerate(steps):
-            for task in tasks_of[i]:
-                round_w(i, task)
-                e = task[0]
-                if task[1] == PASSES - 1 and task[3] == N and e + W_BUFS <= SHARED:
-                    if e + W_BUFS == SHARED:
-                        load_gate(0)
-                    load_w(e + W_BUFS)
-                    if e + W_BUFS == SHARED:
-                        load_gate(1)
-            if step in units:
+                keys = [("W", place[piece_of(e, g, h)][0]) for g in range(PASSES)]
+                keys += [("L", steps.index((e if e == SHARED else e // 2, g))) for g in range(PASSES)]
+                ready = max(quantized.index(key) for key in keys)
+                due[e, h] = quantized[ready + LAG if ready + LAG < quantized.index(("L", len(routed) - 1)) else ready]
+
+        round_plane(0, nc.vector.tensor_copy)
+        for q in range(1, PLANES):
+            round_plane(q, nc.scalar.copy)
+        first = []
+        for kind, i in v_order:
+            if kind == "G":
                 gather(i, 0)
                 gather(i, 1)
-            if step:
-                lay_columns(i)
-            quantize(i)
-            if i < 2:
-                round_plane(4 + i, nc.scalar.copy)
-            for h in range(HALVES):
-                for e in range(E + 1):
-                    if due[e, h] == i:
-                        multiply(e, h)
-            if i == max(due[e, 0] for e in range(E)):
-                first = [fetch(0, r) for r in range(TOP)]
+            elif kind == "F":
+                assert all(v_order.index(due[e, 0]) < v_order.index((kind, i)) for e in range(E))
+                first.append(fetch(0, i))
+            else:
+                if kind == "W":
+                    stage_w(i)
+                else:
+                    stage_columns(i)
+                quantize((kind, i))
+                for h in range(HALVES):
+                    for e in range(E + 1):
+                        if due[e, h] == (kind, i):
+                            multiply(e, h)
 
-        back = sum_on_tensor(first + [ys[:, 0, :]], 0)
-        result = ring.tile([P, T], F32, name="result", bufs=2)
+        second = [fetch(1, r) for r in range(2)]
+        back = sum_on_tensor(first + [ys[:, 0, :]])
+        result = sum_pool.tile([P, T], F32, name="sum_sb")
         nc.scalar.copy(out=result[:], in_=back[:])
         nc.sync.dma_start(out=out[0:P, :], in_=result[:])
-        back = sum_on_tensor([fetch(1, 0), fetch(1, 1), ys[:, 1, :]], 1)
-        total = add(fetch(1, 2)[:], fetch(1, 3)[:])
-        result = ring.tile([P, T], F32, name="result", bufs=2)
+        back = sum_on_tensor(second + [ys[:, 1, :]])
+        third, fourth = fetch(1, 2), fetch(1, 3)
+        total = vector_tile([P, T], F32)
+        result = vector_tile([P, T], F32)
+        for m in range(0, T, T // 2):
+            nc.vector.tensor_tensor(total[:, m : m + T // 2], third[:, m : m + T // 2], fourth[:, m : m + T // 2], ADD)
         for m in range(0, T, T // 2):
             cols = slice(m, m + T // 2)
             nc.vector.tensor_tensor(result[:, cols], back[:, cols], total[:, cols], ADD)

from contextlib import ExitStack

import concourse.mybir as mybir
from concourse.masks import make_identity

K, T, E, C, N, TOP = 1536, 512, 8, 256, 256, 4
FLOPS = 2 * K * N * (E * C + T)

F32 = mybir.dt.float32
BF16 = mybir.dt.bfloat16
U32 = mybir.dt.uint32
U16 = mybir.dt.uint16
U8 = mybir.dt.uint8
FP8X4 = mybir.dt.float8_e4m3fn_x4
SILU = mybir.ActivationFunctionType.Silu
MULT = mybir.AluOpType.mult
ADD = mybir.AluOpType.add

P = 128
PACK = 4
K_PASS = P * PACK
PASSES = K // K_PASS
PLANES = 2 * PASSES
GROUP = 2 * C
HALVES = N // P
SHARED = E
RAW_BUFS = 14
L_RING = 5
W_RING = 3
VECTOR_BUFS = 26
FIRST_SPLIT = 8
UNITS = [[0,0],[1,0],[0,1],[0,2],[1,1],[2,0],[1,2],[3,0],[2,1],[2,2],[3,2],[3,1]]
W_SIZE = [512,512,512,512,512,512,512,512,512,512,512,512,512,256]
ON_GPSIMD = [0,1,3,4,5,7,8,10,11,12]
V_ORDER = "G0 G1 G2 L0 G3 G4 L1 W0 W1 G5 W2 L2 G6 W3 W4 L3 G7 L4 L5 W5 L6 G8 W6 W7 W8 G9 G10 L7 W9 W10 G11 L8 W11 L9 L10 L11 L12 L13 W12 F0 F1 L14 W13 F2 F3"
LAG = 3
GATE_AT = [21,27]


def tile_moe_shr_lin_silu_kernel(tc, xT, w, b, gate, offs, pos1, pos2, pos3, pos4, out):
    nc = tc.nc
    routed = [tuple(u) for u in UNITS]
    steps = routed + [(SHARED, g) for g in range(PASSES)]
    pieces = [(e, g, 0, N if e < FIRST_SPLIT else P) for e in range(E) for g in range(PASSES)]
    pieces += [(e, g, P, N) for e in range(FIRST_SPLIT, E) for g in range(PASSES)]
    pieces += [(SHARED, g, 0, N) for g in range(PASSES)]
    place, width = {}, [0] * len(W_SIZE)
    j = 0
    for piece in pieces:
        while width[j] + piece[3] - piece[2] > W_SIZE[j]:
            j += 1
        place[piece] = (j, width[j])
        width[j] += piece[3] - piece[2]

    with ExitStack() as ctx:
        keep = ctx.enter_context(tc.tile_pool(name="keep", bufs=1))
        raw_pool = ctx.enter_context(tc.tile_pool(name="raw", bufs=RAW_BUFS))
        sum_pool = ctx.enter_context(tc.tile_pool(name="sums", bufs=2))
        vector_pool = ctx.enter_context(tc.tile_pool(name="vector", bufs=VECTOR_BUFS))
        psum = ctx.enter_context(tc.psum_pool(name="psum", bufs=8))

        offs_sb = keep.tile([P, E * C // 16], U16, name="offs_sb")
        pos_sb = [keep.tile([P, T // 16], U16, name="pos_sb%d" % r) for r in range(TOP)]
        bias = keep.tile([P, HALVES, E + 1], F32, name="bias")
        pairs = keep.tile([P, PLANES * T * 2], BF16, name="pairs", align_bytes=64)
        y = [keep.tile([P, E * C], F32, name="y%d" % h) for h in range(HALVES)]
        ys = keep.tile([P, HALVES, T], F32, name="ys")
        l_ring = keep.tile([P, L_RING, GROUP * PACK], BF16, name="l_ring", align_bytes=64)
        w_ring = keep.tile([P, W_RING, GROUP * PACK], BF16, name="w_ring", align_bytes=64)
        ident = keep.tile([P, P], F32, name="ident")
        warm = keep.tile([P, 2], F32, name="warm")

        x_raw, w_raw, gates, gathered, staged, coded = {}, {}, {}, {}, {}, {}

        def vector_tile(shape, dtype):
            return vector_pool.tile(shape, dtype, name="vector_out", align_bytes=64)

        def plane_start(q):
            return (PLANES - 1 - q) * T

        def load_x(q):
            g, u = divmod(q, 2)
            x_raw[q] = raw_pool.tile([P, 2, T], F32, name="raw")
            rows = xT[g * K_PASS : (g + 1) * K_PASS, :].rearrange("(p j) t -> p j t", j=PACK)
            nc.sync.dma_start(out=x_raw[q][:], in_=rows[:, 2 * u : 2 * u + 2, :])

        def load_w(e, g):
            w_raw[e, g] = raw_pool.tile([P, PACK, N], F32, name="raw")
            rows = w[e, g * K_PASS : (g + 1) * K_PASS, :]
            nc.sync.dma_start(out=w_raw[e, g][:], in_=rows.rearrange("(p j) n -> p j n", j=PACK))

        def load_gate(h):
            for a in range(TOP // 2):
                gates[h, a] = raw_pool.tile([P, 2, T], F32, name="raw")
                nc.sync.dma_start(
                    out=gates[h, a][:], in_=gate[2 * a : 2 * a + 2, h * P : (h + 1) * P, :].rearrange("r p t -> p r t")
                )

        def round_plane(q, copy):
            dst = pairs[:, 2 * plane_start(q) : 2 * (plane_start(q) + T)].rearrange("p (t e) -> p t e", e=2)
            copy(out=dst, in_=x_raw[q][:].rearrange("p e t -> p t e"))

        def gather(i, u):
            s, g = steps[i]
            if u == 0:
                gathered[i] = vector_tile([P, 2, GROUP], U32)
            q = 2 * g + u
            columns, count = (T, C) if q == 0 else (2 * T, GROUP)
            window = pairs[:, 2 * plane_start(q) : 2 * (plane_start(q) + columns)].bitcast(U32)
            for m in range(0, GROUP, count):
                cols = slice((s * GROUP + m) // 16, (s * GROUP + m + count) // 16)
                nc.vector.tensor_copy(out=gathered[i][:, u, m : m + count], in_=window.indirect(offs_sb[:, cols]))

        def stage_w(j):
            staged["W", j] = w_ring[:, j % W_RING, : width[j] * PACK]
            for piece in [piece for piece in pieces if place[piece][0] == j]:
                e, g, n0, n1 = piece
                at = place[piece][1] * PACK
                dst, src = staged["W", j][:, at : at + (n1 - n0) * PACK], w_raw[e, g][:, :, n0:n1]
                if j in ON_GPSIMD and place[piece][1] >= N:
                    nc.gpsimd.tensor_scalar(
                        out=dst.rearrange("p (n j) -> p n j", j=PACK),
                        in0=src.rearrange("p j n -> p n j"),
                        scalar1=1.0,
                        scalar2=0.0,
                        op0=MULT,
                        op1=ADD,
                    )
                else:
                    nc.scalar.copy(
                        out=dst.rearrange("p (c i j) -> p c j i", i=4, j=PACK),
                        in_=src.rearrange("p j (c i) -> p c j i", i=4),
                    )

        def stage_columns(i):
            s, g = steps[i]
            staged["L", i] = l_ring[:, i % L_RING, :]
            if s == SHARED:
                both = pairs[:, 2 * plane_start(2 * g + 1) : 2 * (plane_start(2 * g) + T)].bitcast(F32)
                src = both.rearrange("p (u t) -> p t u", u=2)[:, :, ::-1]
            else:
                src = gathered[i][:].bitcast(F32).rearrange("p u m -> p m u")
            nc.scalar.copy(out=staged["L", i].bitcast(F32).rearrange("p (m u) -> p m u", u=2), in_=src)

        def operand(key, at, columns):
            total = staged[key].shape[1] // PACK
            codes = coded[key][:, 4 * at : 4 * (at + columns)].bitcast(FP8X4)
            return codes, coded[key][:, 4 * total + at : 4 * total + at + columns]

        def quantize(key):
            total = staged[key].shape[1] // PACK
            coded[key] = vector_tile([P, 5 * total], U8)
            done = 0
            while done < total:
                columns = max(n for n in (P, N, GROUP) if n <= total - done)
                codes, scales = operand(key, done, columns)
                nc.vector.quantize_mx(out=codes, scales=scales, in_=staged[key][:, done * PACK : (done + columns) * PACK])
                done += columns

        def piece_of(e, g, h):
            return [piece for piece in pieces if piece[:2] == (e, g) and piece[2] <= h * P < piece[3]][0]

        def multiply(e, h):
            columns = T if e == SHARED else C
            acc = psum.tile([P, columns], F32, name="bank")
            for g in range(PASSES):
                piece = piece_of(e, g, h)
                w_codes, w_scales = operand(("W", place[piece][0]), place[piece][1] + h * P - piece[2], P)
                if e == SHARED:
                    x_codes, x_scales = operand(("L", steps.index((SHARED, g))), 0, T)
                else:
                    x_codes, x_scales = operand(("L", steps.index((e // 2, g))), e % 2 * C, C)
                nc.tensor.matmul_mx(
                    out=acc[:],
                    lhsT=w_codes,
                    lhsT_scale=w_scales,
                    rhs=x_codes,
                    rhs_scale=x_scales,
                    start=(g == 0),
                    stop=(g == PASSES - 1),
                )
            dst = ys[:, h, :] if e == SHARED else y[h][:, e * C : (e + 1) * C]
            nc.scalar.activation(out=dst, in_=acc[:], func=SILU, bias=bias[:, h, e : e + 1])

        def fetch(h, r):
            picked = vector_tile([P, T], F32)
            nc.vector.tensor_tensor(picked[:], y[h][:].indirect(pos_sb[r][:]), gates[h, r // 2][:, r % 2, :], MULT)
            return picked

        def sum_on_tensor(terms):
            turned = psum.tile([P, T], F32, name="bank")
            for m in range(0, T, P):
                for k, term in enumerate(terms):
                    nc.tensor.matmul(
                        turned[:, m : m + P],
                        lhsT=term[:, m : m + P],
                        rhs=ident[:],
                        start=(k == 0),
                        stop=(k == len(terms) - 1),
                        is_transpose=True,
                    )
            turned_sb = sum_pool.tile([P, T], F32, name="sum_sb")
            nc.scalar.copy(out=turned_sb[:], in_=turned[:])
            back = psum.tile([P, T], F32, name="bank")
            for m in range(0, T, P):
                nc.tensor.transpose(back[:, m : m + P], turned_sb[:, m : m + P], ident[:])
            return back

        make_identity(nc, ident[:])
        nc.gpsimd.memset(warm[:, 0:1], 0.0)
        nc.scalar.activation(out=warm[:, 1:2], in_=warm[:, 0:1], func=SILU)
        load_x(0)
        nc.sync.dma_start(offs_sb[:], offs)
        for q in range(1, PLANES):
            load_x(q)
        for m in range((E + 1) * PASSES):
            load_w(*divmod(m, PASSES))
            if m == PASSES - 1:
                nc.sync.dma_start(out=bias[:], in_=b.rearrange("(h p) e -> p h e", p=P))
                for r, pos in enumerate((pos1, pos2, pos3, pos4)):
                    nc.sync.dma_start(pos_sb[r][:], pos)
            for h in range(HALVES):
                if m + 1 == GATE_AT[h]:
                    load_gate(h)

        v_order = [(word[0], int(word[1:])) for word in V_ORDER.split()]
        quantized = [key for key in v_order if key[0] in "WL"]
        due = {}
        for e in range(E + 1):
            for h in range(HALVES):
                keys = [("W", place[piece_of(e, g, h)][0]) for g in range(PASSES)]
                keys += [("L", steps.index((e if e == SHARED else e // 2, g))) for g in range(PASSES)]
                ready = max(quantized.index(key) for key in keys)
                due[e, h] = quantized[ready + LAG if ready + LAG < quantized.index(("L", len(routed) - 1)) else ready]

        round_plane(0, nc.vector.tensor_copy)
        for q in range(1, PLANES):
            round_plane(q, nc.scalar.copy)
        first = []
        for kind, i in v_order:
            if kind == "G":
                gather(i, 0)
                gather(i, 1)
            elif kind == "F":
                assert all(v_order.index(due[e, 0]) < v_order.index((kind, i)) for e in range(E))
                first.append(fetch(0, i))
            else:
                if kind == "W":
                    stage_w(i)
                else:
                    stage_columns(i)
                quantize((kind, i))
                for h in range(HALVES):
                    for e in range(E + 1):
                        if due[e, h] == (kind, i):
                            multiply(e, h)

        second = [fetch(1, r) for r in range(2)]
        back = sum_on_tensor(first + [ys[:, 0, :]])
        result = sum_pool.tile([P, T], F32, name="sum_sb")
        nc.scalar.copy(out=result[:], in_=back[:])
        nc.sync.dma_start(out=out[0:P, :], in_=result[:])
        back = sum_on_tensor(second + [ys[:, 1, :]])
        third, fourth = fetch(1, 2), fetch(1, 3)
        total = vector_tile([P, T], F32)
        result = vector_tile([P, T], F32)
        for m in range(0, T, T // 2):
            nc.vector.tensor_tensor(total[:, m : m + T // 2], third[:, m : m + T // 2], fourth[:, m : m + T // 2], ADD)
        for m in range(0, T, T // 2):
            cols = slice(m, m + T // 2)
            nc.vector.tensor_tensor(result[:, cols], back[:, cols], total[:, cols], ADD)
            nc.sync.dma_start(out=out[P : 2 * P, cols], in_=result[:, cols])
